import numpy as np
import ml_dtypes


def mxq(x, axis, fmt="e4m3"):
    dtype, down = {"e4m3": (ml_dtypes.float8_e4m3fn, 7), "e5m2": (ml_dtypes.float8_e5m2, 14)}[fmt]
    v = np.moveaxis(np.asarray(x, np.float32).astype(ml_dtypes.bfloat16).astype(np.float64), axis, -1)
    blocks = v.reshape(v.shape[:-1] + (-1, 32))
    amax = np.abs(blocks).max(-1, keepdims=True)
    byte = np.maximum(np.where(amax > 0, np.frexp(amax)[1] - 1 + 127, 0) - down, 1)
    scale = np.exp2(byte - 127.0)
    codes = (blocks / scale).astype(np.float32).astype(dtype).astype(np.float64)
    return np.moveaxis((codes * scale).reshape(v.shape), -1, axis)


WIDE = False


def mx_kscale(k):
    if not WIDE:
        return np.ones(k)
    levels = np.array([10, -10, 5, -5, 0])
    if k % 512:
        return np.exp2(np.random.permutation(np.resize(levels, k // 32))).repeat(32)
    a = np.empty((k // 512, 16))
    for p in range(k // 512):
        a[p, :8] = np.random.permutation(np.resize(levels, 8))
        for g in range(8):
            far = levels[np.abs(levels - a[p, g]) >= 10]
            a[p, g + 8] = far[np.random.randint(len(far))]
    return np.exp2(a.ravel()).repeat(32)


def f64(x):
    return np.asarray(x).astype(np.float64)


def striped(idx):
    return np.tile(np.asarray(idx).reshape(-1, 16).T, (8, 1)).astype(np.uint16)


def unstriped(offs):
    return offs[:16].T.reshape(-1).astype(np.int64)


E2M1 = np.array([0.0, 0.5, 1.0, 1.5, 2.0, 3.0, 4.0, 6.0, -0.0, -0.5, -1.0, -1.5, -2.0, -3.0, -4.0, -6.0])


def pack_weight(w, fmt):
    k, n = w.shape
    w = f64(np.asarray(w, np.float32).astype(ml_dtypes.bfloat16)).reshape(k // 32, 32, n)
    amax = np.abs(w).max(1)
    if fmt == "e4m3":
        byte = np.frexp(amax)[1] - 1 + 127 - 7
    else:
        mant, ex = np.frexp(amax / 6.0)
        byte = np.where(mant > 0.5, ex, ex - 1) + 127
    byte = np.clip(np.where(amax > 0, byte, 1), 1, 254)
    scaled = (w * np.exp2(127.0 - byte)[:, None, :]).reshape(k, n).astype(np.float32)
    by_word = np.ascontiguousarray(scaled.reshape(k // 512, 128, 4, n).transpose(0, 1, 3, 2))
    if fmt == "e4m3":
        words = by_word.astype(ml_dtypes.float8_e4m3fn).view(np.uint8)
    else:
        c = by_word.astype(ml_dtypes.float4_e2m1fn).view(np.uint8) & 0xF
        words = (c[..., 0::2] | (c[..., 1::2] << 4)).reshape(k // 512, 128, 2 * n)
    return np.ascontiguousarray(words), np.ascontiguousarray(byte.astype(np.uint8).reshape(k // 512, 16, n))


def unpack_weight(words, scales, fmt):
    g, _, n = scales.shape
    words = np.ascontiguousarray(words).reshape(g, 128, n, -1)
    if fmt == "e4m3":
        vals = words.view(ml_dtypes.float8_e4m3fn).astype(np.float64)
    else:
        nib = np.empty((g, 128, n, 4), np.uint8)
        nib[..., 0::2] = words & 0xF
        nib[..., 1::2] = words >> 4
        vals = E2M1[nib]
    vals = vals * np.repeat(np.exp2(scales.astype(np.float64) - 127.0), 8, axis=1)[..., None]
    return vals.transpose(0, 1, 3, 2).reshape(g * 512, n)


K, Q, I, C, J, N = 512, 128, 256, 512, 256, 256


def setup_inputs():
    n = np.random.standard_normal
    idx = np.random.permutation(C)[:I]
    idx2 = np.random.permutation(C)[:I]
    idx3 = np.random.permutation(C)[:J]
    idx4 = np.random.permutation(C)[:J]
    fk = mx_kscale(K)
    wp = pack_weight(n((K, N)) * 1 / np.sqrt(K) / fk[:, None], "e2m1")
    return {
        "ca": (np.random.randint(-7, 8, (Q, I)).astype(np.float64)).astype(np.float32),
        "ga": (np.random.uniform(0.1, 0.4, (Q, 1)) * fk[::4, None]).astype(np.float32),
        "cb": (np.random.randint(-7, 8, (Q, I)).astype(np.float64)).astype(np.float32),
        "gb": (np.random.uniform(0.1, 0.4, (Q, 1)) * fk[::4, None]).astype(np.float32),
        "cc": (np.random.randint(-7, 8, (Q, I)).astype(np.float64)).astype(np.float32),
        "gc": (np.random.uniform(0.1, 0.4, (Q, 1)) * fk[::4, None]).astype(np.float32),
        "cd": (np.random.randint(-7, 8, (Q, I)).astype(np.float64)).astype(np.float32),
        "gd": (np.random.uniform(0.1, 0.4, (Q, 1)) * fk[::4, None]).astype(np.float32),
        "w_words": wp[0],
        "w_scales": wp[1],
        "offs": striped(idx),
        "offs2": striped(idx2),
        "offs3": striped(idx3),
        "offs4": striped(idx4),
    }


def reference(ca, ga, cb, gb, cc, gc, cd, gd, w_words, w_scales, offs, offs2, offs3, offs4):
    idx = unstriped(offs)
    idx2 = unstriped(offs2)
    idx3 = unstriped(offs3)
    idx4 = unstriped(offs4)
    wu = unpack_weight(w_words, w_scales, "e2m1")
    p0 = np.zeros((Q, C))
    p0[:, idx] = f64(ca) * f64(ga)
    p1 = np.zeros((Q, C))
    p1[:, idx] = f64(cb) * f64(gb)
    p2 = np.zeros((Q, C))
    p2[:, idx2] = f64(cc) * f64(gc)
    p3 = np.zeros((Q, C))
    p3[:, idx2] = f64(cd) * f64(gd)
    v0 = p0[:, idx3]
    v1 = p1[:, idx4]
    v2 = p2[:, idx3]
    v3 = p3[:, idx4]
    z = np.stack([v0, v1, v2, v3], axis=1).reshape(K, J)
    zq = mxq(z, 0, "e4m3")
    p = wu.T @ zq
    return p

@@ -1,0 +1,90 @@
+from contextlib import ExitStack
+
+import concourse.mybir as mybir
+
+F32 = mybir.dt.float32
+BF16 = mybir.dt.bfloat16
+I32 = mybir.dt.int32
+U32 = mybir.dt.uint32
+U16 = mybir.dt.uint16
+U8 = mybir.dt.uint8
+FP8X4 = mybir.dt.float8_e4m3fn_x4
+FP4X4 = mybir.dt.float4_e2m1fn_x4
+COPY = mybir.ActivationFunctionType.Copy
+
+P = 128
+K, CODES, PAGE, CASES, N = 512, 256, 512, 256, 256
+HALF = 128
+FLOPS = 2 * K * N * CASES
+
+
+def tile_list_fourpages_kernel(tc, ca, ga, cb, gb, cc, gc, cd, gd, w_words, w_scales, offs, offs2, offs3, offs4, out):
+    nc = tc.nc
+    with ExitStack() as ctx:
+        keep = ctx.enter_context(tc.tile_pool(name="keep", bufs=1))
+        psum = ctx.enter_context(tc.psum_pool(name="psum", bufs=1))
+
+        lists = [keep.tile([P, 16], U16, name="list%d" % t) for t in range(4)]
+        codes = [keep.tile([P, CODES], F32, name="codes%d" % t) for t in range(4)]
+        steps = [keep.tile([P, 1], F32, name="steps%d" % t) for t in range(4)]
+        pages = [keep.tile([P, PAGE], F32, name="page%d" % t) for t in range(4)]
+        w_sb = keep.tile([P, 2 * N], U8, align_bytes=64)
+        w_rows = keep.tile([4, 4, N // 4], I32)
+        w_plane = keep.tile([P, N], U8, align_bytes=64)
+        zs = [keep.tile([P, 4 * HALF], BF16, name="z%d" % h, align_bytes=64) for h in range(2)]
+        zc = [keep.tile([P, HALF], U32, name="zc%d" % h, align_bytes=64) for h in range(2)]
+        zp = [keep.tile([P, HALF], U8, name="zp%d" % h, align_bytes=64) for h in range(2)]
+
+        nc.scalar.dma_start(steps[0][:], ga)
+        nc.sync.dma_start(lists[0][:], offs)
+        nc.sync.dma_start(codes[0][:], ca)
+        nc.sync.dma_start(steps[1][:], gb)
+        nc.sync.dma_start(codes[1][:], cb)
+        nc.sync.dma_start(lists[1][:], offs2)
+        nc.sync.dma_start(steps[2][:], gc)
+        nc.sync.dma_start(codes[2][:], cc)
+        nc.sync.dma_start(steps[3][:], gd)
+        nc.sync.dma_start(codes[3][:], cd)
+        nc.sync.dma_start(w_rows[:], w_scales[0].bitcast(I32).rearrange("(q r) c -> r q c", r=4))
+        nc.sync.dma_start(w_sb[:].bitcast(I32), w_words[0].bitcast(I32))
+        nc.sync.dma_start(lists[2][:], offs3)
+        nc.sync.dma_start(lists[3][:], offs4)
+
+        for t in range(4):
+            nc.vector.memset(pages[t][:], 0.0)
+        nc.vector.memset(w_plane[:].bitcast(I32), 0)
+        for q in range(4):
+            nc.vector.tensor_copy(out=w_plane[32 * q : 32 * q + 4, :].bitcast(I32), in_=w_rows[:, q, :])
+
+        for t in range(4):
+            nc.scalar.activation(out=pages[t][:].indirect(lists[t // 2][:]), in_=codes[t][:], func=COPY, scale=steps[t][:])
+
+        for h in range(2):
+            cols = slice(h * HALF, (h + 1) * HALF)
+            for t in range(4):
+                nc.scalar.activation(
+                    out=zs[h][:, t : 4 * HALF : 4],
+                    in_=pages[t][:].indirect(lists[2 + t % 2][:, 8 * h : 8 * h + 8]),
+                    func=COPY,
+                )
+            nc.vector.quantize_mx(
+                out=zc[h][:].bitcast(FP8X4), scales=zp[h][:], in_=zs[h][:]
+            )
+            for m in range(2):
+                acc = psum.tile([P, HALF], F32, name="acc%d%d" % (h, m))
+                nc.tensor.matmul_mx(
+                    out=acc[:],
+                    lhsT=w_sb[:, 2 * m * P : 2 * (m + 1) * P].bitcast(FP4X4),
+                    lhsT_scale=w_plane[:, m * P : (m + 1) * P],
+                    rhs=zc[h][:].bitcast(FP8X4),
+                    rhs_scale=zp[h][:],
+                    start=True,
+                    stop=True,
+                )
+                res = keep.tile([P, HALF], F32, name="res%d%d" % (h, m))
+                if h == 1 and m == 1:
+                    nc.scalar.copy(out=res[:], in_=acc[:])
+                    nc.scalar.dma_start(out[m * P : (m + 1) * P, cols], res[:])
+                else:
+                    nc.vector.tensor_copy(out=res[:], in_=acc[:])
+                    nc.sync.dma_start(out[m * P : (m + 1) * P, cols], res[:])

@@ -50,6 +50,11 @@ def tile_list_fourpages_kernel(tc, ca, ga, cb, gb, cc, gc, cd, gd, w_words, w_sc
         nc.sync.dma_start(lists[2][:], offs3)
         nc.sync.dma_start(lists[3][:], offs4)
 
+        warm_in = keep.tile([P, 1], F32)
+        warm_out = keep.tile([P, 1], F32)
+        nc.gpsimd.memset(warm_in[:], 0.0)
+        nc.scalar.activation(out=warm_out[:], in_=warm_in[:], func=COPY)
+
         for t in range(4):
             nc.vector.memset(pages[t][:], 0.0)
         nc.vector.memset(w_plane[:].bitcast(I32), 0)

@@ -31,13 +31,13 @@ def tile_list_fourpages_kernel(tc, ca, ga, cb, gb, cc, gc, cd, gd, w_words, w_sc
         w_sb = keep.tile([P, 2 * N], U8, align_bytes=64)
         w_rows = keep.tile([4, 4, N // 4], I32)
         w_plane = keep.tile([P, N], U8, align_bytes=64)
-        zs = [keep.tile([P, 4 * HALF], BF16, name="z%d" % h, align_bytes=64) for h in range(2)]
-        zc = [keep.tile([P, HALF], U32, name="zc%d" % h, align_bytes=64) for h in range(2)]
-        zp = [keep.tile([P, HALF], U8, name="zp%d" % h, align_bytes=64) for h in range(2)]
+        z = keep.tile([P, 4 * CASES], BF16, align_bytes=64)
+        z_codes = keep.tile([P, CASES], U32, align_bytes=64)
+        z_plane = keep.tile([P, CASES], U8, align_bytes=64)
 
-        nc.scalar.dma_start(steps[0][:], ga)
+        nc.scalar.dma_start(codes[0][:], ca)
+        nc.sync.dma_start(steps[0][:], ga)
         nc.sync.dma_start(lists[0][:], offs)
-        nc.sync.dma_start(codes[0][:], ca)
         nc.sync.dma_start(steps[1][:], gb)
         nc.sync.dma_start(codes[1][:], cb)
         nc.sync.dma_start(lists[1][:], offs2)
@@ -52,7 +52,7 @@ def tile_list_fourpages_kernel(tc, ca, ga, cb, gb, cc, gc, cd, gd, w_words, w_sc
 
         warm_in = keep.tile([P, 1], F32)
         warm_out = keep.tile([P, 1], F32)
-        nc.gpsimd.memset(warm_in[:], 0.0)
+        nc.vector.memset(warm_in[:], 0.0)
         nc.scalar.activation(out=warm_out[:], in_=warm_in[:], func=COPY)
 
         for t in range(4):
@@ -64,32 +64,45 @@ def tile_list_fourpages_kernel(tc, ca, ga, cb, gb, cc, gc, cd, gd, w_words, w_sc
         for t in range(4):
             nc.scalar.activation(out=pages[t][:].indirect(lists[t // 2][:]), in_=codes[t][:], func=COPY, scale=steps[t][:])
 
+        def fetch(t, first, count):
+            nc.scalar.activation(
+                out=z[:, 4 * first + t : 4 * (first + count) : 4],
+                in_=pages[t][:].indirect(lists[2 + t % 2][:, first // 16 : (first + count) // 16]),
+                func=COPY,
+            )
+
+        def multiply(h, m):
+            cols = slice(h * HALF, (h + 1) * HALF)
+            acc = psum.tile([P, HALF], F32, name="acc%d%d" % (h, m))
+            nc.tensor.matmul_mx(
+                out=acc[:],
+                lhsT=w_sb[:, 2 * m * P : 2 * (m + 1) * P].bitcast(FP4X4),
+                lhsT_scale=w_plane[:, m * P : (m + 1) * P],
+                rhs=z_codes[:, cols].bitcast(FP8X4),
+                rhs_scale=z_plane[:, cols],
+                start=True,
+                stop=True,
+            )
+            return acc
+
+        for t in (0, 2):
+            fetch(t, 0, CASES)
         for h in range(2):
             cols = slice(h * HALF, (h + 1) * HALF)
-            for t in range(4):
-                nc.scalar.activation(
-                    out=zs[h][:, t : 4 * HALF : 4],
-                    in_=pages[t][:].indirect(lists[2 + t % 2][:, 8 * h : 8 * h + 8]),
-                    func=COPY,
-                )
+            for t in (1, 3):
+                fetch(t, h * HALF, HALF)
             nc.vector.quantize_mx(
-                out=zc[h][:].bitcast(FP8X4), scales=zp[h][:], in_=zs[h][:]
+                out=z_codes[:, cols].bitcast(FP8X4), scales=z_plane[:, cols], in_=z[:, 4 * h * HALF : 4 * (h + 1) * HALF]
             )
-            for m in range(2):
-                acc = psum.tile([P, HALF], F32, name="acc%d%d" % (h, m))
-                nc.tensor.matmul_mx(
-                    out=acc[:],
-                    lhsT=w_sb[:, 2 * m * P : 2 * (m + 1) * P].bitcast(FP4X4),
-                    lhsT_scale=w_plane[:, m * P : (m + 1) * P],
-                    rhs=zc[h][:].bitcast(FP8X4),
-                    rhs_scale=zp[h][:],
-                    start=True,
-                    stop=True,
-                )
-                res = keep.tile([P, HALF], F32, name="res%d%d" % (h, m))
-                if h == 1 and m == 1:
-                    nc.scalar.copy(out=res[:], in_=acc[:])
-                    nc.scalar.dma_start(out[m * P : (m + 1) * P, cols], res[:])
-                else:
-                    nc.vector.tensor_copy(out=res[:], in_=acc[:])
-                    nc.sync.dma_start(out[m * P : (m + 1) * P, cols], res[:])
+            if h == 0:
+                res_a = keep.tile([P, 2, HALF], F32)
+                nc.vector.tensor_copy(out=res_a[:, 0, :], in_=multiply(0, 0)[:])
+                nc.scalar.copy(out=res_a[:, 1, :], in_=multiply(0, 1)[:])
+                nc.sync.dma_start(out[:, cols].rearrange("(m p) c -> p m c", p=P), res_a[:])
+            else:
+                res_b1 = keep.tile([P, HALF], F32)
+                nc.vector.tensor_copy(out=res_b1[:], in_=multiply(1, 1)[:])
+                nc.sync.dma_start(out[P : 2 * P, cols], res_b1[:])
+                res_b0 = keep.tile([P, HALF], F32)
+                nc.scalar.copy(out=res_b0[:], in_=multiply(1, 0)[:])
+                nc.scalar.dma_start(out[0:P, cols], res_b0[:])

@@ -96,7 +96,7 @@ def tile_list_fourpages_kernel(tc, ca, ga, cb, gb, cc, gc, cd, gd, w_words, w_sc
             )
             if h == 0:
                 res_a = keep.tile([P, 2, HALF], F32)
-                nc.vector.tensor_copy(out=res_a[:, 0, :], in_=multiply(0, 0)[:])
+                nc.scalar.copy(out=res_a[:, 0, :], in_=multiply(0, 0)[:])
                 nc.scalar.copy(out=res_a[:, 1, :], in_=multiply(0, 1)[:])
                 nc.sync.dma_start(out[:, cols].rearrange("(m p) c -> p m c", p=P), res_a[:])
             else:

from contextlib import ExitStack

import concourse.mybir as mybir

F32 = mybir.dt.float32
BF16 = mybir.dt.bfloat16
I32 = mybir.dt.int32
U32 = mybir.dt.uint32
U16 = mybir.dt.uint16
U8 = mybir.dt.uint8
FP8X4 = mybir.dt.float8_e4m3fn_x4
FP4X4 = mybir.dt.float4_e2m1fn_x4
COPY = mybir.ActivationFunctionType.Copy

P = 128
K, CODES, PAGE, CASES, N = 512, 256, 512, 256, 256
HALF = 128
FLOPS = 2 * K * N * CASES


def tile_list_fourpages_kernel(tc, ca, ga, cb, gb, cc, gc, cd, gd, w_words, w_scales, offs, offs2, offs3, offs4, out):
    nc = tc.nc
    with ExitStack() as ctx:
        keep = ctx.enter_context(tc.tile_pool(name="keep", bufs=1))
        psum = ctx.enter_context(tc.psum_pool(name="psum", bufs=1))

        lists = [keep.tile([P, 16], U16, name="list%d" % t) for t in range(4)]
        codes = [keep.tile([P, CODES], F32, name="codes%d" % t) for t in range(4)]
        steps = [keep.tile([P, 1], F32, name="steps%d" % t) for t in range(4)]
        pages = [keep.tile([P, PAGE], F32, name="page%d" % t) for t in range(4)]
        w_sb = keep.tile([P, 2 * N], U8, align_bytes=64)
        w_rows = keep.tile([4, 4, N // 4], I32)
        w_plane = keep.tile([P, N], U8, align_bytes=64)
        z = keep.tile([P, 4 * CASES], BF16, align_bytes=64)
        z_codes = keep.tile([P, CASES], U32, align_bytes=64)
        z_plane = keep.tile([P, CASES], U8, align_bytes=64)

        nc.scalar.dma_start(codes[0][:], ca)
        nc.sync.dma_start(steps[0][:], ga)
        nc.sync.dma_start(lists[0][:], offs)
        nc.sync.dma_start(steps[1][:], gb)
        nc.sync.dma_start(codes[1][:], cb)
        nc.sync.dma_start(lists[1][:], offs2)
        nc.sync.dma_start(steps[2][:], gc)
        nc.sync.dma_start(codes[2][:], cc)
        nc.sync.dma_start(steps[3][:], gd)
        nc.sync.dma_start(codes[3][:], cd)
        nc.sync.dma_start(w_rows[:], w_scales[0].bitcast(I32).rearrange("(q r) c -> r q c", r=4))
        nc.sync.dma_start(w_sb[:].bitcast(I32), w_words[0].bitcast(I32))
        nc.sync.dma_start(lists[2][:], offs3)
        nc.sync.dma_start(lists[3][:], offs4)

        warm_in = keep.tile([P, 1], F32)
        warm_out = keep.tile([P, 1], F32)
        nc.vector.memset(warm_in[:], 0.0)
        nc.scalar.activation(out=warm_out[:], in_=warm_in[:], func=COPY)

        for t in range(4):
            nc.vector.memset(pages[t][:], 0.0)
        nc.vector.memset(w_plane[:].bitcast(I32), 0)
        for q in range(4):
            nc.vector.tensor_copy(out=w_plane[32 * q : 32 * q + 4, :].bitcast(I32), in_=w_rows[:, q, :])

        for t in range(4):
            nc.scalar.activation(out=pages[t][:].indirect(lists[t // 2][:]), in_=codes[t][:], func=COPY, scale=steps[t][:])

        def fetch(t, first, count):
            nc.scalar.activation(
                out=z[:, 4 * first + t : 4 * (first + count) : 4],
                in_=pages[t][:].indirect(lists[2 + t % 2][:, first // 16 : (first + count) // 16]),
                func=COPY,
            )

        def multiply(h, m):
            cols = slice(h * HALF, (h + 1) * HALF)
            acc = psum.tile([P, HALF], F32, name="acc%d%d" % (h, m))
            nc.tensor.matmul_mx(
                out=acc[:],
                lhsT=w_sb[:, 2 * m * P : 2 * (m + 1) * P].bitcast(FP4X4),
                lhsT_scale=w_plane[:, m * P : (m + 1) * P],
                rhs=z_codes[:, cols].bitcast(FP8X4),
                rhs_scale=z_plane[:, cols],
                start=True,
                stop=True,
            )
            return acc

        for t in (0, 2):
            fetch(t, 0, CASES)
        for h in range(2):
            cols = slice(h * HALF, (h + 1) * HALF)
            for t in (1, 3):
                fetch(t, h * HALF, HALF)
            nc.vector.quantize_mx(
                out=z_codes[:, cols].bitcast(FP8X4), scales=z_plane[:, cols], in_=z[:, 4 * h * HALF : 4 * (h + 1) * HALF]
            )
            if h == 0:
                res_a = keep.tile([P, 2, HALF], F32)
                nc.scalar.copy(out=res_a[:, 0, :], in_=multiply(0, 0)[:])
                nc.scalar.copy(out=res_a[:, 1, :], in_=multiply(0, 1)[:])
                nc.sync.dma_start(out[:, cols].rearrange("(m p) c -> p m c", p=P), res_a[:])
            else:
                res_b1 = keep.tile([P, HALF], F32)
                nc.vector.tensor_copy(out=res_b1[:], in_=multiply(1, 1)[:])
                nc.sync.dma_start(out[P : 2 * P, cols], res_b1[:])
                res_b0 = keep.tile([P, HALF], F32)
                nc.scalar.copy(out=res_b0[:], in_=multiply(1, 0)[:])
                nc.scalar.dma_start(out[0:P, cols], res_b0[:])
